import numpy as np
import ml_dtypes


def mxq(x, axis, fmt="e4m3"):
    dtype, down = {"e4m3": (ml_dtypes.float8_e4m3fn, 7), "e5m2": (ml_dtypes.float8_e5m2, 14)}[fmt]
    v = np.moveaxis(np.asarray(x, np.float32).astype(ml_dtypes.bfloat16).astype(np.float64), axis, -1)
    blocks = v.reshape(v.shape[:-1] + (-1, 32))
    amax = np.abs(blocks).max(-1, keepdims=True)
    byte = np.maximum(np.where(amax > 0, np.frexp(amax)[1] - 1 + 127, 0) - down, 1)
    scale = np.exp2(byte - 127.0)
    codes = (blocks / scale).astype(np.float32).astype(dtype).astype(np.float64)
    return np.moveaxis((codes * scale).reshape(v.shape), -1, axis)


WIDE = False


def mx_kscale(k):
    if not WIDE:
        return np.ones(k)
    levels = np.array([10, -10, 5, -5, 0])
    if k % 512:
        return np.exp2(np.random.permutation(np.resize(levels, k // 32))).repeat(32)
    a = np.empty((k // 512, 16))
    for p in range(k // 512):
        a[p, :8] = np.random.permutation(np.resize(levels, 8))
        for g in range(8):
            far = levels[np.abs(levels - a[p, g]) >= 10]
            a[p, g + 8] = far[np.random.randint(len(far))]
    return np.exp2(a.ravel()).repeat(32)


def f64(x):
    return np.asarray(x).astype(np.float64)


def striped(idx):
    return np.tile(idx.reshape(-1, 16).T, (8, 1)).astype(np.uint16)


def unstriped(offs):
    return offs[:16].T.reshape(-1).astype(np.int64)


E2M1 = np.array([0.0, 0.5, 1.0, 1.5, 2.0, 3.0, 4.0, 6.0, -0.0, -0.5, -1.0, -1.5, -2.0, -3.0, -4.0, -6.0])


def pack_weight(w, fmt):
    k, n = w.shape
    w = f64(np.asarray(w, np.float32).astype(ml_dtypes.bfloat16)).reshape(k // 32, 32, n)
    amax = np.abs(w).max(1)
    if fmt == "e4m3":
        byte = np.frexp(amax)[1] - 1 + 127 - 7
    else:
        mant, ex = np.frexp(amax / 6.0)
        byte = np.where(mant > 0.5, ex, ex - 1) + 127
    byte = np.clip(np.where(amax > 0, byte, 1), 1, 254)
    scaled = (w * np.exp2(127.0 - byte)[:, None, :]).reshape(k, n).astype(np.float32)
    by_word = np.ascontiguousarray(scaled.reshape(k // 512, 128, 4, n).transpose(0, 1, 3, 2))
    if fmt == "e4m3":
        words = by_word.astype(ml_dtypes.float8_e4m3fn).view(np.uint8)
    else:
        c = by_word.astype(ml_dtypes.float4_e2m1fn).view(np.uint8) & 0xF
        words = (c[..., 0::2] | (c[..., 1::2] << 4)).reshape(k // 512, 128, 2 * n)
    return np.ascontiguousarray(words), np.ascontiguousarray(byte.astype(np.uint8).reshape(k // 512, 16, n))


def unpack_weight(words, scales, fmt):
    g, _, n = scales.shape
    words = np.ascontiguousarray(words).reshape(g, 128, n, -1)
    if fmt == "e4m3":
        vals = words.view(ml_dtypes.float8_e4m3fn).astype(np.float64)
    else:
        nib = np.empty((g, 128, n, 4), np.uint8)
        nib[..., 0::2] = words & 0xF
        nib[..., 1::2] = words >> 4
        vals = E2M1[nib]
    vals = vals * np.repeat(np.exp2(scales.astype(np.float64) - 127.0), 8, axis=1)[..., None]
    return vals.transpose(0, 1, 3, 2).reshape(g * 512, n)


def gelu(v):
    return 0.5 * v * (1.0 + np.tanh(np.sqrt(2.0 / np.pi) * (v + 0.044715 * v**3)))


def striped8(idx):
    return np.concatenate([v.reshape(-1, 16).T for v in idx]).astype(np.uint16)


def unstriped8(offs):
    return np.stack([offs[16 * g:16 * g + 16].T.reshape(-1) for g in range(8)]).astype(np.int64)


def runs(v, idx8):
    k = np.arange(v.shape[0])
    return v[k[:, None], idx8[k % 512 // 64]]


K, H, N, T, S, P = 1024, 1024, 384, 2048, 1024, 512


def setup_inputs():
    n = np.random.standard_normal
    s = mx_kscale(K)[:, None]
    u = mx_kscale(H)[:, None]
    d = {}
    d["tab_words"], d["tab_scales"] = pack_weight(n((K, T)) * s, "e4m3")
    d["offs"] = striped8(np.stack([np.random.permutation(T)[:S] for _ in range(8)]))
    d["pos1"] = striped(np.random.permutation(S)[:P])
    d["pos2"] = striped(np.random.permutation(S)[:P])
    d["w1"] = (n((K, H)) / K ** 0.5 / s).astype(np.float32)
    d["w2_words"], d["w2_scales"] = pack_weight(1.6 * n((K, H)) / K ** 0.5 / s, "e2m1")
    d["gain"] = (np.exp(0.3 * n(H)) * u[:, 0]).astype(np.float32)
    d["w3"] = (1.6 * n((H, N)) / H ** 0.5 / u).astype(np.float32)
    return d


def reference(tab_words, tab_scales, offs, pos1, pos2, w1, w2_words, w2_scales, gain, w3):
    v = runs(unpack_weight(tab_words, tab_scales, "e4m3"), unstriped8(offs))
    w2 = unpack_weight(w2_words, w2_scales, "e2m1")
    a = mxq(f64(w1), 0, "e4m3").T @ v
    b = w2.T @ v
    h = a + np.tanh(b)
    h1 = h[:, unstriped(pos1)]
    h2 = h[:, unstriped(pos2)]
    z = h1 * np.exp(-np.abs(h2)) * f64(gain)[:, None]
    out = mxq(f64(w3), 0, "e4m3").T @ mxq(z, 0, "e4m3")
    return out

@@ -1,0 +1,316 @@
+from contextlib import ExitStack
+
+import concourse.mybir as mybir
+
+K, H, N, T, S, P = 1024, 1024, 384, 2048, 1024, 512
+FLOPS = 2 * (2 * K * H * S + H * N * P)
+
+F32 = mybir.dt.float32
+BF16 = mybir.dt.bfloat16
+I32 = mybir.dt.int32
+U32 = mybir.dt.uint32
+U16 = mybir.dt.uint16
+U8 = mybir.dt.uint8
+FP8X4 = mybir.dt.float8_e4m3fn_x4
+FP4X4 = mybir.dt.float4_e2m1fn_x4
+ACT = mybir.ActivationFunctionType
+ALU = mybir.AluOpType
+
+PARTS = 128
+PACK = 4
+K_PASS = PARTS * PACK
+RUN = 4
+BANK = 512
+K_PASSES = K // K_PASS
+R_PASSES = H // K_PASS
+TILES = R_PASSES * PACK
+N_TILES = N // PARTS
+
+
+def tile_list_ply_splice_uniformity_kernel(tc, tab_words, tab_scales, offs, pos1, pos2, w1, w2_words, w2_scales, gain, w3, out):
+    nc = tc.nc
+    with ExitStack() as ctx:
+        lists = ctx.enter_context(tc.tile_pool(name="lists", bufs=1))
+        keep = ctx.enter_context(tc.tile_pool(name="keep", bufs=1))
+        work = ctx.enter_context(tc.tile_pool(name="work", bufs=2))
+        psum = ctx.enter_context(tc.psum_pool(name="psum", bufs=1))
+
+        offs_t = lists.tile([PARTS, S // 16], U16, name="offs_t")
+        pos1_t = lists.tile([PARTS, P // 16], U16, name="pos1_t")
+        pos2_t = lists.tile([PARTS, P // 16], U16, name="pos2_t")
+        nc.sync.dma_start(offs_t[:], offs)
+        nc.sync.dma_start(pos1_t[:], pos1)
+        nc.sync.dma_start(pos2_t[:], pos2)
+
+        scale_window = keep.tile([PARTS, T], U8, name="scale_window", tag="slot_a", align_bytes=64)
+        nc.gpsimd.memset(scale_window[:].bitcast(I32), 0)
+        for a in range(K_PASSES):
+            nc.scalar.dma_start(scale_window[:].bitcast(I32)[4 * a : PARTS : 8, :], tab_scales[a].bitcast(I32))
+
+        warm = keep.tile([PARTS, 8], F32, name="warm")
+        nc.gpsimd.memset(warm[:, 0:1], 0.0)
+        nc.scalar.activation(warm[:, 4:5], warm[:, 0:1], ACT.Exp)
+
+        word_windows = []
+        for a in range(K_PASSES):
+            window = keep.tile([PARTS, T], I32, name="word_window%d" % a, tag="slot_w%d" % a, align_bytes=64)
+            nc.sync.dma_start(window[:], tab_words[a].rearrange("p t i -> p (t i)").bitcast(I32))
+            word_windows.append(window)
+
+        w2_raw = keep.tile([PARTS, K_PASSES * H // 2], I32, name="w2_raw", tag="slot_c", align_bytes=64)
+        nc.sync.dma_start(
+            w2_raw[:].rearrange("p (a c) -> p a c", a=K_PASSES),
+            w2_words.bitcast(I32).rearrange("a p c -> p a c"),
+        )
+        w2s_raw = keep.tile([PARTS, K_PASSES * H // 4], I32, name="w2s_raw", align_bytes=64)
+        nc.gpsimd.memset(w2s_raw[:], 0)
+        for d in range(4):
+            nc.gpsimd.dma_start(
+                w2s_raw[32 * d : 32 * d + 4, :].rearrange("r (a c) -> r a c", a=K_PASSES),
+                w2_scales.bitcast(I32)[:, 4 * d : 4 * d + 4, :].rearrange("a r c -> r a c"),
+            )
+        gain_t = keep.tile([PARTS, R_PASSES, 16], F32, name="gain_t")
+        for w in range(RUN):
+            nc.gpsimd.dma_start(
+                gain_t[w:PARTS:RUN, :, 0:13],
+                gain.rearrange("(b i x) -> i b x", b=R_PASSES, x=16)[:, :, w : w + 13],
+            )
+
+        w1_raw = {}
+
+        def load_w1(a, b, tag):
+            raw = keep.tile([PARTS, PACK, K_PASS], F32, name="w1_raw%d%d" % (a, b), tag=tag, align_bytes=64)
+            nc.sync.dma_start(
+                raw[:],
+                w1[K_PASS * a : K_PASS * (a + 1), K_PASS * b : K_PASS * (b + 1)].rearrange("(p j) c -> p j c", j=PACK),
+            )
+            w1_raw[a, b] = raw
+
+        v_scales = []
+        for a in range(K_PASSES):
+            plane = keep.tile([PARTS, S], U8, name="v_scales%d" % a, align_bytes=64)
+            nc.vector.memset(plane[:].bitcast(I32), 0)
+            v_scales.append(plane)
+        picked_scales = keep.tile([PARTS, S], U8, name="picked_scales", align_bytes=64)
+        nc.vector.tensor_copy(picked_scales[:], scale_window[:].indirect(offs_t[:]))
+        for a in range(K_PASSES):
+            for r in range(4):
+                nc.scalar.dma_start(
+                    v_scales[a][:].bitcast(I32)[r:PARTS:32, :],
+                    picked_scales[:].bitcast(I32)[8 * r + 4 * a : PARTS : 32, :],
+                )
+        load_w1(0, 0, "slot_a")
+
+        v_words = []
+        for a in range(K_PASSES):
+            words = keep.tile([PARTS, S], U32, name="v_words%d" % a, align_bytes=64)
+            nc.vector.tensor_copy(words[:], word_windows[a][:].bitcast(U32).indirect(offs_t[:]))
+            v_words.append(words)
+
+        w2_codes = keep.tile([PARTS, K_PASSES * H * 2], U8, name="w2_codes", align_bytes=64)
+        nc.vector.tensor_copy(
+            w2_codes[:].bitcast(I32).rearrange("p (g t i x) -> p g t i x", t=PACK, i=32, x=2),
+            w2_raw[:].rearrange("p (g i t x) -> p g t i x", t=PACK, i=32, x=2),
+        )
+        w2_planes = keep.tile([PARTS, K_PASSES * H], U8, name="w2_planes", align_bytes=64)
+        nc.vector.tensor_copy(
+            w2_planes[:].bitcast(I32).rearrange("p (g t i x) -> p g i t x", t=PACK, i=8, x=4),
+            w2s_raw[:].rearrange("p (g i x t) -> p g i t x", t=PACK, i=8, x=4),
+        )
+
+        load_w1(1, 0, "slot_w0")
+        load_w1(0, 1, "slot_w1")
+        load_w1(1, 1, "slot_c")
+
+        w3_raw = {}
+
+        def load_w3(b, tag):
+            raw = keep.tile([PARTS, PACK, N], F32, name="w3_raw%d" % b, tag=tag, align_bytes=64)
+            rows = w3[K_PASS * b : K_PASS * (b + 1), :].rearrange("(i t w) n -> w i t n", t=PACK, w=RUN)
+            for w in range(RUN):
+                nc.sync.dma_start(raw[w:PARTS:RUN, :, :], rows[w])
+            w3_raw[b] = raw
+
+        w1_grouped = [keep.tile([PARTS, K_PASSES * K_PASS], BF16, name="w1_grouped%d" % n, align_bytes=64) for n in range(TILES)]
+        w1_q = {}
+
+        def round_w1(a, n, copy):
+            b, t = divmod(n, PACK)
+            copy(
+                w1_grouped[n][:, K_PASS * a : K_PASS * (a + 1)].rearrange("p (i w j) -> p i j w", w=RUN, j=PACK),
+                w1_raw[a, b][:].rearrange("p j (i t w) -> p t i j w", t=PACK, w=RUN)[:, t],
+            )
+
+        def quantise_w1(n):
+            codes = keep.tile([PARTS, K_PASSES * PARTS], U32, name="w1_codes%d" % n, align_bytes=64)
+            scales = keep.tile([PARTS, K_PASSES * PARTS], U8, name="w1_scales%d" % n, align_bytes=64)
+            nc.vector.quantize_mx(out=codes[:].bitcast(FP8X4), scales=scales[:], in_=w1_grouped[n][:])
+            w1_q[n] = (codes, scales)
+
+        halves = [slice(BANK * half, BANK * (half + 1)) for half in range(S // BANK)]
+        tanh_b = {}
+
+        def bounded_part(n):
+            tanh_b[n] = work.tile([PARTS, S], F32, name="tanh_b")
+            for cols in halves:
+                bank = psum.tile([PARTS, BANK], F32, name="bounded", bufs=4)
+                for a in range(K_PASSES):
+                    c0 = PARTS * (TILES * a + n)
+                    nc.tensor.matmul_mx(
+                        out=bank[:],
+                        lhsT=w2_codes[:, 2 * c0 : 2 * (c0 + PARTS)].bitcast(FP4X4),
+                        lhsT_scale=w2_planes[:, c0 : c0 + PARTS],
+                        rhs=v_words[a][:, cols].bitcast(FP8X4),
+                        rhs_scale=v_scales[a][:, cols],
+                        start=(a == 0),
+                        stop=(a == K_PASSES - 1),
+                    )
+                nc.scalar.activation(tanh_b[n][:, cols], bank[:], ACT.Tanh)
+
+        h_tiles = {}
+        opposite = {}
+
+        def features(n, pair_ranges):
+            codes, scales = w1_q[n]
+            h = work.tile([PARTS, S], F32, name="h", bufs=3)
+            for cols in halves:
+                bank = psum.tile([PARTS, BANK], F32, name="linear", bufs=4)
+                for a in range(K_PASSES):
+                    nc.tensor.matmul_mx(
+                        out=bank[:],
+                        lhsT=codes[:, PARTS * a : PARTS * (a + 1)].bitcast(FP8X4),
+                        lhsT_scale=scales[:, PARTS * a : PARTS * (a + 1)],
+                        rhs=v_words[a][:, cols].bitcast(FP8X4),
+                        rhs_scale=v_scales[a][:, cols],
+                        start=(a == 0),
+                        stop=(a == K_PASSES - 1),
+                    )
+                nc.vector.tensor_tensor(h[:, cols], bank[:], tanh_b[n][:, cols], ALU.add)
+            h_tiles[n] = h
+            for m0, m1 in pair_ranges:
+                h2 = work.tile([PARTS, m1 - m0], F32, name="h2", bufs=3)
+                nc.vector.tensor_copy(h2[:], h[:].indirect(pos2_t[:, m0 // 16 : m1 // 16]))
+                opposite[n, m0] = h2
+
+        z_f32 = [keep.tile([PARTS, PACK * P], F32, name="z_f32_%d" % b) for b in range(R_PASSES)]
+
+        def damp(n, pair_ranges):
+            b, t = divmod(n, PACK)
+            for m0, m1 in pair_ranges:
+                size = work.tile([PARTS, m1 - m0], F32, name="size")
+                nc.scalar.activation(size[:], opposite[n, m0][:], ACT.Abs)
+                decay = work.tile([PARTS, m1 - m0], F32, name="decay")
+                nc.scalar.activation(decay[:], size[:], ACT.Exp, scale=-1.0)
+                factor = work.tile([PARTS, m1 - m0], F32, name="factor")
+                nc.scalar.activation(factor[:], decay[:], ACT.Copy, scale=gain_t[:, b, RUN * t : RUN * t + 1])
+                nc.vector.tensor_tensor(
+                    z_f32[b][:, P * t + m0 : P * t + m1],
+                    h_tiles[n][:].indirect(pos1_t[:, m0 // 16 : m1 // 16]),
+                    factor[:],
+                    ALU.mult,
+                )
+
+        w3_grouped = [keep.tile([PARTS, N * PACK], BF16, name="w3_grouped%d" % b, align_bytes=64) for b in range(R_PASSES)]
+        w3_q = {}
+
+        def round_w3(b, k):
+            nc.scalar.copy(
+                w3_grouped[b][:, K_PASS * k : K_PASS * (k + 1)].rearrange("p (c x t) -> p c t x", x=4, t=PACK),
+                w3_raw[b][:, :, PARTS * k : PARTS * (k + 1)].rearrange("p t (c x) -> p c t x", x=4),
+            )
+
+        def quantise_w3(b):
+            codes = work.tile([PARTS, N], U32, name="w3_codes", align_bytes=64)
+            scales = work.tile([PARTS, N], U8, name="w3_scales", align_bytes=64)
+            for c0, c1 in ((0, 256), (256, N)):
+                nc.vector.quantize_mx(
+                    out=codes[:, c0:c1].bitcast(FP8X4), scales=scales[:, c0:c1], in_=w3_grouped[b][:, PACK * c0 : PACK * c1]
+                )
+            w3_q[b] = (codes, scales)
+
+        z_grouped = [keep.tile([PARTS, P * PACK], BF16, name="z_grouped%d" % b, align_bytes=64) for b in range(R_PASSES)]
+        z_codes = [keep.tile([PARTS, P], U32, name="z_codes%d" % b, align_bytes=64) for b in range(R_PASSES)]
+        z_scales = [keep.tile([PARTS, P], U8, name="z_scales%d" % b, align_bytes=64) for b in range(R_PASSES)]
+
+        def round_z(b, m0, m1, copy):
+            copy(
+                z_grouped[b][:, PACK * m0 : PACK * m1].rearrange("p (c x t) -> p c t x", x=4, t=PACK),
+                z_f32[b][:].rearrange("p (t m) -> p t m", t=PACK)[:, :, m0:m1].rearrange("p t (c x) -> p c t x", x=4),
+            )
+
+        def quantise_z(b, m0, m1):
+            nc.vector.quantize_mx(
+                out=z_codes[b][:, m0:m1].bitcast(FP8X4), scales=z_scales[b][:, m0:m1], in_=z_grouped[b][:, PACK * m0 : PACK * m1]
+            )
+
+        def second_product(scores, b, m0, m1, start, stop):
+            for k in range(N_TILES):
+                cols = slice(PARTS * k, PARTS * (k + 1))
+                nc.tensor.matmul_mx(
+                    out=scores[k][:, m0:m1],
+                    lhsT=w3_q[b][0][:, cols].bitcast(FP8X4),
+                    lhsT_scale=w3_q[b][1][:, cols],
+                    rhs=z_codes[b][:, m0:m1].bitcast(FP8X4),
+                    rhs_scale=z_scales[b][:, m0:m1],
+                    start=start,
+                    stop=stop,
+                )
+
+        whole = [(0, P)]
+        split = [(0, P // 2), (P // 2, P)]
+        last = TILES - 1
+
+        for n in range(PACK):
+            round_w1(0, n, nc.scalar.copy)
+        load_w3(0, "slot_a")
+        bounded_part(0)
+        for n in range(2):
+            round_w1(1, n, nc.vector.tensor_copy)
+            quantise_w1(n)
+        features(0, whole)
+        bounded_part(1)
+        for n in range(2, PACK):
+            round_w1(1, n, nc.scalar.copy)
+            quantise_w1(n)
+        load_w3(1, "slot_w0")
+        features(1, whole)
+        spare = [lambda n=n: round_w1(0, n, nc.scalar.copy) for n in (4, 5)]
+        for job in spare:
+            job()
+        jobs = [(1, 4), (0, 6), (1, 5), (0, 7), (1, 6), (1, 7)]
+        w3_jobs = [(b, k) for b in range(R_PASSES) for k in range(N_TILES)]
+        for n in range(2, TILES):
+            damp(n - 2, whole)
+            bounded_part(n)
+            features(n, split if n == last else whole)
+            step = n - 2
+            for a, m in jobs[2 * step : 2 * step + 2]:
+                round_w1(a, m, nc.scalar.copy)
+                if a == 1:
+                    quantise_w1(m)
+            if step >= 3:
+                for b, k in w3_jobs[2 * (step - 3) : 2 * (step - 3) + 2]:
+                    round_w3(b, k)
+                    if k == N_TILES - 1:
+                        quantise_w3(b)
+            if n == last - 1:
+                round_z(0, P // 2, P, nc.vector.tensor_copy)
+        damp(last - 1, whole)
+        scores = [psum.tile([PARTS, P], F32, name="scores%d" % k, tag="bounded", bufs=4) for k in range(N_TILES)]
+        round_z(0, 0, P // 2, nc.scalar.copy)
+        quantise_z(0, 0, P)
+        second_product(scores, 0, 0, P, True, False)
+        damp(last, split)
+        round_z(1, 0, P // 2, nc.scalar.copy)
+        round_z(1, P // 2, P, nc.vector.tensor_copy)
+        quantise_z(1, P // 2, P)
+        second_product(scores, 1, P // 2, P, False, False)
+        quantise_z(1, 0, P // 2)
+        second_product(scores, 1, 0, P // 2, False, True)
+        for k in range(N_TILES):
+            result = work.tile([PARTS, P], F32, name="result", bufs=3)
+            if k == 1:
+                nc.scalar.copy(result[:], scores[k][:])
+            else:
+                nc.vector.tensor_copy(result[:], scores[k][:])
+            nc.sync.dma_start(out[PARTS * k : PARTS * (k + 1), :], result[:])

@@ -32,6 +32,7 @@ def tile_list_ply_splice_uniformity_kernel(tc, tab_words, tab_scales, offs, pos1
     with ExitStack() as ctx:
         lists = ctx.enter_context(tc.tile_pool(name="lists", bufs=1))
         keep = ctx.enter_context(tc.tile_pool(name="keep", bufs=1))
+        placed = ctx.enter_context(tc.tile_pool(name="placed", bufs=1))
         work = ctx.enter_context(tc.tile_pool(name="work", bufs=2))
         psum = ctx.enter_context(tc.psum_pool(name="psum", bufs=1))
 
@@ -39,29 +40,45 @@ def tile_list_ply_splice_uniformity_kernel(tc, tab_words, tab_scales, offs, pos1
         pos1_t = lists.tile([PARTS, P // 16], U16, name="pos1_t")
         pos2_t = lists.tile([PARTS, P // 16], U16, name="pos2_t")
         nc.sync.dma_start(offs_t[:], offs)
+        word_windows = [
+            placed.tile([PARTS, T], I32, name="word_window0", offset=8128, align_bytes=64),
+            keep.tile([PARTS, T], I32, name="word_window1", tag="slot_w1", align_bytes=64),
+        ]
+        for a in range(K_PASSES):
+            nc.sync.dma_start(word_windows[a][:], tab_words[a].rearrange("p t i -> p (t i)").bitcast(I32))
         nc.sync.dma_start(pos1_t[:], pos1)
         nc.sync.dma_start(pos2_t[:], pos2)
 
+        warm_in = keep.tile([PARTS, 1], F32, name="warm_in", tag="slot_d", align_bytes=64)
+        warm_out = keep.tile([PARTS, 1], F32, name="warm_out", tag="slot_c", align_bytes=64)
+
         scale_window = keep.tile([PARTS, T], U8, name="scale_window", tag="slot_a", align_bytes=64)
-        nc.gpsimd.memset(scale_window[:].bitcast(I32), 0)
-        for a in range(K_PASSES):
-            nc.scalar.dma_start(scale_window[:].bitcast(I32)[4 * a : PARTS : 8, :], tab_scales[a].bitcast(I32))
+        nc.vector.memset(scale_window[:].bitcast(I32), 0)
+        nc.vector.memset(warm_in[:], 0.0)
+        for e in range(2):
+            nc.scalar.dma_start(
+                scale_window[:].bitcast(I32)[e:PARTS:16, :],
+                tab_scales[0].bitcast(I32).rearrange("(g e) c -> e g c", e=2)[e],
+            )
+        nc.scalar.dma_start(scale_window[:].bitcast(I32)[4:PARTS:8, :], tab_scales[1].bitcast(I32))
+        nc.scalar.activation(warm_out[:], warm_in[:], ACT.Exp)
 
-        warm = keep.tile([PARTS, 8], F32, name="warm")
-        nc.gpsimd.memset(warm[:, 0:1], 0.0)
-        nc.scalar.activation(warm[:, 4:5], warm[:, 0:1], ACT.Exp)
+        w1_raw = {}
 
-        word_windows = []
-        for a in range(K_PASSES):
-            window = keep.tile([PARTS, T], I32, name="word_window%d" % a, tag="slot_w%d" % a, align_bytes=64)
-            nc.sync.dma_start(window[:], tab_words[a].rearrange("p t i -> p (t i)").bitcast(I32))
-            word_windows.append(window)
+        def load_w1(a, b, pool, **place):
+            raw = pool.tile([PARTS, PACK, K_PASS], F32, name="w1_raw%d%d" % (a, b), align_bytes=64, **place)
+            nc.sync.dma_start(
+                raw[:],
+                w1[K_PASS * a : K_PASS * (a + 1), K_PASS * b : K_PASS * (b + 1)].rearrange("(p j) c -> p j c", j=PACK),
+            )
+            w1_raw[a, b] = raw
 
         w2_raw = keep.tile([PARTS, K_PASSES * H // 2], I32, name="w2_raw", tag="slot_c", align_bytes=64)
         nc.sync.dma_start(
             w2_raw[:].rearrange("p (a c) -> p a c", a=K_PASSES),
             w2_words.bitcast(I32).rearrange("a p c -> p a c"),
         )
+        load_w1(0, 0, keep, tag="slot_d")
         w2s_raw = keep.tile([PARTS, K_PASSES * H // 4], I32, name="w2s_raw", align_bytes=64)
         nc.gpsimd.memset(w2s_raw[:], 0)
         for d in range(4):
@@ -69,69 +86,67 @@ def tile_list_ply_splice_uniformity_kernel(tc, tab_words, tab_scales, offs, pos1
                 w2s_raw[32 * d : 32 * d + 4, :].rearrange("r (a c) -> r a c", a=K_PASSES),
                 w2_scales.bitcast(I32)[:, 4 * d : 4 * d + 4, :].rearrange("a r c -> r a c"),
             )
-        gain_t = keep.tile([PARTS, R_PASSES, 16], F32, name="gain_t")
+
+        v_scales = [keep.tile([PARTS, S], U8, name="v_scales%d" % a, align_bytes=64) for a in range(K_PASSES)]
+        nc.vector.memset(v_scales[1][:].bitcast(I32), 0)
+        v_words = [
+            keep.tile([PARTS, S], U32, name="v_words0", align_bytes=64),
+            keep.tile([PARTS, S], U32, name="v_words1", tag="slot_a", align_bytes=64),
+        ]
+        nc.vector.tensor_copy(v_words[0][:], word_windows[0][:].bitcast(U32).indirect(offs_t[:]))
+        load_w1(1, 0, placed, offset=0)
+        picked_scales = placed.tile([PARTS, S], U8, name="picked_scales", offset=15872, align_bytes=64)
+        nc.vector.tensor_copy(picked_scales[:], scale_window[:].indirect(offs_t[:]))
+        nc.vector.tensor_copy(v_scales[0][:].bitcast(I32), picked_scales[:].bitcast(I32))
+        for r in range(4):
+            nc.scalar.dma_start(
+                v_scales[1][:].bitcast(I32)[r:PARTS:32, :], picked_scales[:].bitcast(I32)[8 * r + 4 : PARTS : 32, :]
+            )
+        for e in range(2):
+            nc.scalar.dma_start(
+                v_scales[0][:].bitcast(I32)[2 + e : PARTS : 32, :], picked_scales[:].bitcast(I32)[16 + e : PARTS : 32, :]
+            )
+        nc.vector.tensor_copy(v_words[1][:], word_windows[1][:].bitcast(U32).indirect(offs_t[:]))
+        gain_t = keep.tile([PARTS, R_PASSES, 16], F32, name="gain_t", tag="slot_w1", align_bytes=64)
         for w in range(RUN):
-            nc.gpsimd.dma_start(
+            nc.sync.dma_start(
                 gain_t[w:PARTS:RUN, :, 0:13],
                 gain.rearrange("(b i x) -> i b x", b=R_PASSES, x=16)[:, :, w : w + 13],
             )
 
-        w1_raw = {}
-
-        def load_w1(a, b, tag):
-            raw = keep.tile([PARTS, PACK, K_PASS], F32, name="w1_raw%d%d" % (a, b), tag=tag, align_bytes=64)
-            nc.sync.dma_start(
-                raw[:],
-                w1[K_PASS * a : K_PASS * (a + 1), K_PASS * b : K_PASS * (b + 1)].rearrange("(p j) c -> p j c", j=PACK),
-            )
-            w1_raw[a, b] = raw
-
-        v_scales = []
-        for a in range(K_PASSES):
-            plane = keep.tile([PARTS, S], U8, name="v_scales%d" % a, align_bytes=64)
-            nc.vector.memset(plane[:].bitcast(I32), 0)
-            v_scales.append(plane)
-        picked_scales = keep.tile([PARTS, S], U8, name="picked_scales", align_bytes=64)
-        nc.vector.tensor_copy(picked_scales[:], scale_window[:].indirect(offs_t[:]))
-        for a in range(K_PASSES):
-            for r in range(4):
-                nc.scalar.dma_start(
-                    v_scales[a][:].bitcast(I32)[r:PARTS:32, :],
-                    picked_scales[:].bitcast(I32)[8 * r + 4 * a : PARTS : 32, :],
-                )
-        load_w1(0, 0, "slot_a")
-
-        v_words = []
-        for a in range(K_PASSES):
-            words = keep.tile([PARTS, S], U32, name="v_words%d" % a, align_bytes=64)
-            nc.vector.tensor_copy(words[:], word_windows[a][:].bitcast(U32).indirect(offs_t[:]))
-            v_words.append(words)
-
-        w2_codes = keep.tile([PARTS, K_PASSES * H * 2], U8, name="w2_codes", align_bytes=64)
-        nc.vector.tensor_copy(
-            w2_codes[:].bitcast(I32).rearrange("p (g t i x) -> p g t i x", t=PACK, i=32, x=2),
-            w2_raw[:].rearrange("p (g i t x) -> p g t i x", t=PACK, i=32, x=2),
-        )
         w2_planes = keep.tile([PARTS, K_PASSES * H], U8, name="w2_planes", align_bytes=64)
         nc.vector.tensor_copy(
             w2_planes[:].bitcast(I32).rearrange("p (g t i x) -> p g i t x", t=PACK, i=8, x=4),
             w2s_raw[:].rearrange("p (g i x t) -> p g i t x", t=PACK, i=8, x=4),
         )
+        w2_source = w2_raw[:].rearrange("p (a b i t x) -> p b t a i x", a=K_PASSES, b=R_PASSES, t=PACK, x=2)
+        w2_codes = {}
 
-        load_w1(1, 0, "slot_w0")
-        load_w1(0, 1, "slot_w1")
-        load_w1(1, 1, "slot_c")
+        def deal_w2(tile, n0, n1):
+            words = tile[:].bitcast(I32).rearrange("p (n a i x) -> p n a i x", a=K_PASSES, i=32, x=2)
+            for b in range(R_PASSES):
+                t0, t1 = max(n0 - PACK * b, 0), min(n1 - PACK * b, PACK)
+                if t0 < t1:
+                    nc.vector.tensor_copy(words[:, PACK * b + t0 - n0 : PACK * b + t1 - n0], w2_source[:, b, t0:t1])
+            for n in range(n0, n1):
+                for a in range(K_PASSES):
+                    c0 = 2 * PARTS * (K_PASSES * (n - n0) + a)
+                    w2_codes[n, a] = tile[:, c0 : c0 + 2 * PARTS]
+
+        deal_w2(keep.tile([PARTS, K_PASSES * 2 * PARTS], U8, name="w2_first", align_bytes=64), 0, 1)
+        load_w1(0, 1, placed, offset=8192)
+        load_w1(1, 1, placed, offset=16384)
 
         w3_raw = {}
 
-        def load_w3(b, tag):
-            raw = keep.tile([PARTS, PACK, N], F32, name="w3_raw%d" % b, tag=tag, align_bytes=64)
+        def load_w3(b, pool, **place):
+            raw = pool.tile([PARTS, PACK, N], F32, name="w3_raw%d" % b, align_bytes=64, **place)
             rows = w3[K_PASS * b : K_PASS * (b + 1), :].rearrange("(i t w) n -> w i t n", t=PACK, w=RUN)
             for w in range(RUN):
                 nc.sync.dma_start(raw[w:PARTS:RUN, :, :], rows[w])
             w3_raw[b] = raw
 
-        w1_grouped = [keep.tile([PARTS, K_PASSES * K_PASS], BF16, name="w1_grouped%d" % n, align_bytes=64) for n in range(TILES)]
+        w1_grouped = [keep.tile([PARTS, K_PASSES * K_PASS], BF16, name="w1_grouped%d" % n, tag="grouped%d" % n, align_bytes=64) for n in range(TILES)]
         w1_q = {}
 
         def round_w1(a, n, copy):
@@ -151,14 +166,17 @@ def tile_list_ply_splice_uniformity_kernel(tc, tab_words, tab_scales, offs, pos1
         tanh_b = {}
 
         def bounded_part(n):
-            tanh_b[n] = work.tile([PARTS, S], F32, name="tanh_b")
+            if n == 0:
+                tanh_b[n] = keep.tile([PARTS, S], F32, name="tanh_first", tag="slot_d", align_bytes=64)
+            else:
+                tanh_b[n] = work.tile([PARTS, S], F32, name="tanh_b")
             for cols in halves:
                 bank = psum.tile([PARTS, BANK], F32, name="bounded", bufs=4)
                 for a in range(K_PASSES):
                     c0 = PARTS * (TILES * a + n)
                     nc.tensor.matmul_mx(
                         out=bank[:],
-                        lhsT=w2_codes[:, 2 * c0 : 2 * (c0 + PARTS)].bitcast(FP4X4),
+                        lhsT=w2_codes[n, a].bitcast(FP4X4),
                         lhsT_scale=w2_planes[:, c0 : c0 + PARTS],
                         rhs=v_words[a][:, cols].bitcast(FP8X4),
                         rhs_scale=v_scales[a][:, cols],
@@ -243,18 +261,24 @@ def tile_list_ply_splice_uniformity_kernel(tc, tab_words, tab_scales, offs, pos1
                 out=z_codes[b][:, m0:m1].bitcast(FP8X4), scales=z_scales[b][:, m0:m1], in_=z_grouped[b][:, PACK * m0 : PACK * m1]
             )
 
-        def second_product(scores, b, m0, m1, start, stop):
+        def second_product(scores, b, m0, m1):
             for k in range(N_TILES):
                 cols = slice(PARTS * k, PARTS * (k + 1))
                 nc.tensor.matmul_mx(
-                    out=scores[k][:, m0:m1],
+                    out=scores[k][:, 0 : m1 - m0],
                     lhsT=w3_q[b][0][:, cols].bitcast(FP8X4),
                     lhsT_scale=w3_q[b][1][:, cols],
                     rhs=z_codes[b][:, m0:m1].bitcast(FP8X4),
                     rhs_scale=z_scales[b][:, m0:m1],
-                    start=start,
-                    stop=stop,
+                    start=(b == 0),
+                    stop=(b == R_PASSES - 1),
                 )
+
+        def store(scores, m0, m1, copies):
+            result = work.tile([PARTS, N_TILES, m1 - m0], F32, name="result")
+            for k in range(N_TILES):
+                copies[k](result[:, k, :], scores[k][:, 0 : m1 - m0])
+            nc.sync.dma_start(out.rearrange("(k p) m -> p k m", p=PARTS)[:, :, m0:m1], result[:])
 
         whole = [(0, P)]
         split = [(0, P // 2), (P // 2, P)]
@@ -262,17 +286,19 @@ def tile_list_ply_splice_uniformity_kernel(tc, tab_words, tab_scales, offs, pos1
 
         for n in range(PACK):
             round_w1(0, n, nc.scalar.copy)
-        load_w3(0, "slot_a")
         bounded_part(0)
         for n in range(2):
             round_w1(1, n, nc.vector.tensor_copy)
             quantise_w1(n)
+            if n == 0:
+                rest = keep.tile([PARTS, (TILES - 1) * K_PASSES * 2 * PARTS], U8, name="w2_rest", tag="grouped0", align_bytes=64)
+                deal_w2(rest, 1, TILES)
         features(0, whole)
         bounded_part(1)
         for n in range(2, PACK):
             round_w1(1, n, nc.scalar.copy)
             quantise_w1(n)
-        load_w3(1, "slot_w0")
+        load_w3(0, placed, offset=0)
         features(1, whole)
         spare = [lambda n=n: round_w1(0, n, nc.scalar.copy) for n in (4, 5)]
         for job in spare:
@@ -288,29 +314,29 @@ def tile_list_ply_splice_uniformity_kernel(tc, tab_words, tab_scales, offs, pos1
                 round_w1(a, m, nc.scalar.copy)
                 if a == 1:
                     quantise_w1(m)
+            if step == 1:
+                load_w3(1, placed, offset=8192)
             if step >= 3:
                 for b, k in w3_jobs[2 * (step - 3) : 2 * (step - 3) + 2]:
                     round_w3(b, k)
                     if k == N_TILES - 1:
                         quantise_w3(b)
             if n == last - 1:
-                round_z(0, P // 2, P, nc.vector.tensor_copy)
+                round_z(0, P // 2, P, nc.scalar.copy)
         damp(last - 1, whole)
-        scores = [psum.tile([PARTS, P], F32, name="scores%d" % k, tag="bounded", bufs=4) for k in range(N_TILES)]
+        scores = [
+            [psum.tile([PARTS, BANK], F32, name="scores_%s%d" % (tag, k), tag=tag, bufs=4) for k in range(N_TILES)]
+            for tag in ("bounded", "linear")
+        ]
         round_z(0, 0, P // 2, nc.scalar.copy)
         quantise_z(0, 0, P)
-        second_product(scores, 0, 0, P, True, False)
+        for half, (m0, m1) in enumerate(split):
+            second_product(scores[half], 0, m0, m1)
         damp(last, split)
         round_z(1, 0, P // 2, nc.scalar.copy)
         round_z(1, P // 2, P, nc.vector.tensor_copy)
-        quantise_z(1, P // 2, P)
-        second_product(scores, 1, P // 2, P, False, False)
-        quantise_z(1, 0, P // 2)
-        second_product(scores, 1, 0, P // 2, False, True)
-        for k in range(N_TILES):
-            result = work.tile([PARTS, P], F32, name="result", bufs=3)
-            if k == 1:
-                nc.scalar.copy(result[:], scores[k][:])
-            else:
-                nc.vector.tensor_copy(result[:], scores[k][:])
-            nc.sync.dma_start(out[PARTS * k : PARTS * (k + 1), :], result[:])
+        for half, (m0, m1) in enumerate(split):
+            quantise_z(1, m0, m1)
+            second_product(scores[half], 1, m0, m1)
+        store(scores[0], 0, P // 2, (nc.scalar.copy, nc.scalar.copy, nc.vector.tensor_copy))
+        store(scores[1], P // 2, P, (nc.vector.tensor_copy, nc.scalar.copy, nc.vector.tensor_copy))

@@ -49,10 +49,10 @@ def tile_list_ply_splice_uniformity_kernel(tc, tab_words, tab_scales, offs, pos1
         nc.sync.dma_start(pos1_t[:], pos1)
         nc.sync.dma_start(pos2_t[:], pos2)
 
-        warm_in = keep.tile([PARTS, 1], F32, name="warm_in", tag="slot_d", align_bytes=64)
-        warm_out = keep.tile([PARTS, 1], F32, name="warm_out", tag="slot_c", align_bytes=64)
+        warm_in = keep.tile([PARTS, 1], F32, name="warm_in", tag="slot_c", align_bytes=64)
+        warm_out = keep.tile([PARTS, 1], F32, name="warm_out", tag="slot_d", align_bytes=64)
 
-        scale_window = keep.tile([PARTS, T], U8, name="scale_window", tag="slot_a", align_bytes=64)
+        scale_window = keep.tile([PARTS, T], U8, name="scale_window", align_bytes=64)
         nc.vector.memset(scale_window[:].bitcast(I32), 0)
         nc.vector.memset(warm_in[:], 0.0)
         for e in range(2):
@@ -91,21 +91,19 @@ def tile_list_ply_splice_uniformity_kernel(tc, tab_words, tab_scales, offs, pos1
         nc.vector.memset(v_scales[1][:].bitcast(I32), 0)
         v_words = [
             keep.tile([PARTS, S], U32, name="v_words0", align_bytes=64),
-            keep.tile([PARTS, S], U32, name="v_words1", tag="slot_a", align_bytes=64),
+            placed.tile([PARTS, S], U32, name="v_words1", offset=12288, align_bytes=64),
         ]
         nc.vector.tensor_copy(v_words[0][:], word_windows[0][:].bitcast(U32).indirect(offs_t[:]))
         load_w1(1, 0, placed, offset=0)
-        picked_scales = placed.tile([PARTS, S], U8, name="picked_scales", offset=15872, align_bytes=64)
+        picked_scales = placed.tile([PARTS, S], U8, name="picked_scales", offset=15360, align_bytes=64)
         nc.vector.tensor_copy(picked_scales[:], scale_window[:].indirect(offs_t[:]))
+        staged = placed.tile([PARTS, S // 4], I32, name="staged", offset=24064, align_bytes=64)
+        nc.vector.tensor_copy(staged[:], picked_scales[:].bitcast(I32))
         nc.vector.tensor_copy(v_scales[0][:].bitcast(I32), picked_scales[:].bitcast(I32))
         for r in range(4):
-            nc.scalar.dma_start(
-                v_scales[1][:].bitcast(I32)[r:PARTS:32, :], picked_scales[:].bitcast(I32)[8 * r + 4 : PARTS : 32, :]
-            )
+            nc.scalar.dma_start(v_scales[1][:].bitcast(I32)[r:PARTS:32, :], staged[8 * r + 4 : PARTS : 32, :])
         for e in range(2):
-            nc.scalar.dma_start(
-                v_scales[0][:].bitcast(I32)[2 + e : PARTS : 32, :], picked_scales[:].bitcast(I32)[16 + e : PARTS : 32, :]
-            )
+            nc.scalar.dma_start(v_scales[0][:].bitcast(I32)[2 + e : PARTS : 32, :], staged[16 + e : PARTS : 32, :])
         nc.vector.tensor_copy(v_words[1][:], word_windows[1][:].bitcast(U32).indirect(offs_t[:]))
         gain_t = keep.tile([PARTS, R_PASSES, 16], F32, name="gain_t", tag="slot_w1", align_bytes=64)
         for w in range(RUN):
@@ -134,8 +132,8 @@ def tile_list_ply_splice_uniformity_kernel(tc, tab_words, tab_scales, offs, pos1
                     w2_codes[n, a] = tile[:, c0 : c0 + 2 * PARTS]
 
         deal_w2(keep.tile([PARTS, K_PASSES * 2 * PARTS], U8, name="w2_first", align_bytes=64), 0, 1)
-        load_w1(0, 1, placed, offset=8192)
-        load_w1(1, 1, placed, offset=16384)
+        load_w1(0, 1, placed, offset=16384)
+        load_w1(1, 1, placed, offset=24576)
 
         w3_raw = {}
 
@@ -157,8 +155,8 @@ def tile_list_ply_splice_uniformity_kernel(tc, tab_words, tab_scales, offs, pos1
             )
 
         def quantise_w1(n):
-            codes = keep.tile([PARTS, K_PASSES * PARTS], U32, name="w1_codes%d" % n, align_bytes=64)
-            scales = keep.tile([PARTS, K_PASSES * PARTS], U8, name="w1_scales%d" % n, align_bytes=64)
+            codes = work.tile([PARTS, K_PASSES * PARTS], U32, name="w1_codes", align_bytes=64)
+            scales = work.tile([PARTS, K_PASSES * PARTS], U8, name="w1_scales", align_bytes=64)
             nc.vector.quantize_mx(out=codes[:].bitcast(FP8X4), scales=scales[:], in_=w1_grouped[n][:])
             w1_q[n] = (codes, scales)
 
@@ -297,32 +295,24 @@ def tile_list_ply_splice_uniformity_kernel(tc, tab_words, tab_scales, offs, pos1
         bounded_part(1)
         for n in range(2, PACK):
             round_w1(1, n, nc.scalar.copy)
-            quantise_w1(n)
-        load_w3(0, placed, offset=0)
+        quantise_w1(2)
+        load_w3(0, keep, tag="slot_c")
+        load_w3(1, placed, offset=0)
         features(1, whole)
-        spare = [lambda n=n: round_w1(0, n, nc.scalar.copy) for n in (4, 5)]
-        for job in spare:
-            job()
-        jobs = [(1, 4), (0, 6), (1, 5), (0, 7), (1, 6), (1, 7)]
-        w3_jobs = [(b, k) for b in range(R_PASSES) for k in range(N_TILES)]
+        quantise_w1(3)
         for n in range(2, TILES):
             damp(n - 2, whole)
             bounded_part(n)
             features(n, split if n == last else whole)
-            step = n - 2
-            for a, m in jobs[2 * step : 2 * step + 2]:
-                round_w1(a, m, nc.scalar.copy)
-                if a == 1:
-                    quantise_w1(m)
-            if step == 1:
-                load_w3(1, placed, offset=8192)
-            if step >= 3:
-                for b, k in w3_jobs[2 * (step - 3) : 2 * (step - 3) + 2]:
-                    round_w3(b, k)
-                    if k == N_TILES - 1:
-                        quantise_w3(b)
-            if n == last - 1:
-                round_z(0, P // 2, P, nc.scalar.copy)
+            if n + 2 < TILES:
+                for a in range(K_PASSES):
+                    round_w1(a, n + 2, nc.scalar.copy)
+                quantise_w1(n + 2)
+            if n >= last - 1:
+                for k in range(N_TILES):
+                    round_w3(n - last + 1, k)
+                quantise_w3(n - last + 1)
+        round_z(0, P // 2, P, nc.vector.tensor_copy)
         damp(last - 1, whole)
         scores = [
             [psum.tile([PARTS, BANK], F32, name="scores_%s%d" % (tag, k), tag=tag, bufs=4) for k in range(N_TILES)]

@@ -155,8 +155,8 @@ def tile_list_ply_splice_uniformity_kernel(tc, tab_words, tab_scales, offs, pos1
             )
 
         def quantise_w1(n):
-            codes = work.tile([PARTS, K_PASSES * PARTS], U32, name="w1_codes", align_bytes=64)
-            scales = work.tile([PARTS, K_PASSES * PARTS], U8, name="w1_scales", align_bytes=64)
+            codes = work.tile([PARTS, K_PASSES * PARTS], U32, name="w1_codes", bufs=4, align_bytes=64)
+            scales = work.tile([PARTS, K_PASSES * PARTS], U8, name="w1_scales", bufs=4, align_bytes=64)
             nc.vector.quantize_mx(out=codes[:].bitcast(FP8X4), scales=scales[:], in_=w1_grouped[n][:])
             w1_q[n] = (codes, scales)
 
@@ -273,10 +273,10 @@ def tile_list_ply_splice_uniformity_kernel(tc, tab_words, tab_scales, offs, pos1
                 )
 
         def store(scores, m0, m1, copies):
-            result = work.tile([PARTS, N_TILES, m1 - m0], F32, name="result")
             for k in range(N_TILES):
-                copies[k](result[:, k, :], scores[k][:, 0 : m1 - m0])
-            nc.sync.dma_start(out.rearrange("(k p) m -> p k m", p=PARTS)[:, :, m0:m1], result[:])
+                result = work.tile([PARTS, m1 - m0], F32, name="result", bufs=2 * N_TILES)
+                copies[k](result[:], scores[k][:, 0 : m1 - m0])
+                nc.sync.dma_start(out[PARTS * k : PARTS * (k + 1), m0:m1], result[:])
 
         whole = [(0, P)]
         split = [(0, P // 2), (P // 2, P)]
@@ -291,15 +291,15 @@ def tile_list_ply_splice_uniformity_kernel(tc, tab_words, tab_scales, offs, pos1
             if n == 0:
                 rest = keep.tile([PARTS, (TILES - 1) * K_PASSES * 2 * PARTS], U8, name="w2_rest", tag="grouped0", align_bytes=64)
                 deal_w2(rest, 1, TILES)
-        features(0, whole)
-        bounded_part(1)
         for n in range(2, PACK):
             round_w1(1, n, nc.scalar.copy)
-        quantise_w1(2)
+        features(0, whole)
+        for n in range(2, PACK):
+            quantise_w1(n)
+        bounded_part(1)
         load_w3(0, keep, tag="slot_c")
         load_w3(1, placed, offset=0)
         features(1, whole)
-        quantise_w1(3)
         for n in range(2, TILES):
             damp(n - 2, whole)
             bounded_part(n)

from contextlib import ExitStack

import concourse.mybir as mybir

K, H, N, T, S, P = 1024, 1024, 384, 2048, 1024, 512
FLOPS = 2 * (2 * K * H * S + H * N * P)

F32 = mybir.dt.float32
BF16 = mybir.dt.bfloat16
I32 = mybir.dt.int32
U32 = mybir.dt.uint32
U16 = mybir.dt.uint16
U8 = mybir.dt.uint8
FP8X4 = mybir.dt.float8_e4m3fn_x4
FP4X4 = mybir.dt.float4_e2m1fn_x4
ACT = mybir.ActivationFunctionType
ALU = mybir.AluOpType

PARTS = 128
PACK = 4
K_PASS = PARTS * PACK
RUN = 4
BANK = 512
K_PASSES = K // K_PASS
R_PASSES = H // K_PASS
TILES = R_PASSES * PACK
N_TILES = N // PARTS


def tile_list_ply_splice_uniformity_kernel(tc, tab_words, tab_scales, offs, pos1, pos2, w1, w2_words, w2_scales, gain, w3, out):
    nc = tc.nc
    with ExitStack() as ctx:
        lists = ctx.enter_context(tc.tile_pool(name="lists", bufs=1))
        keep = ctx.enter_context(tc.tile_pool(name="keep", bufs=1))
        placed = ctx.enter_context(tc.tile_pool(name="placed", bufs=1))
        work = ctx.enter_context(tc.tile_pool(name="work", bufs=2))
        psum = ctx.enter_context(tc.psum_pool(name="psum", bufs=1))

        offs_t = lists.tile([PARTS, S // 16], U16, name="offs_t")
        pos1_t = lists.tile([PARTS, P // 16], U16, name="pos1_t")
        pos2_t = lists.tile([PARTS, P // 16], U16, name="pos2_t")
        nc.sync.dma_start(offs_t[:], offs)
        word_windows = [
            placed.tile([PARTS, T], I32, name="word_window0", offset=8128, align_bytes=64),
            keep.tile([PARTS, T], I32, name="word_window1", tag="slot_w1", align_bytes=64),
        ]
        for a in range(K_PASSES):
            nc.sync.dma_start(word_windows[a][:], tab_words[a].rearrange("p t i -> p (t i)").bitcast(I32))
        nc.sync.dma_start(pos1_t[:], pos1)
        nc.sync.dma_start(pos2_t[:], pos2)

        warm_in = keep.tile([PARTS, 1], F32, name="warm_in", tag="slot_c", align_bytes=64)
        warm_out = keep.tile([PARTS, 1], F32, name="warm_out", tag="slot_d", align_bytes=64)

        scale_window = keep.tile([PARTS, T], U8, name="scale_window", align_bytes=64)
        nc.vector.memset(scale_window[:].bitcast(I32), 0)
        nc.vector.memset(warm_in[:], 0.0)
        for e in range(2):
            nc.scalar.dma_start(
                scale_window[:].bitcast(I32)[e:PARTS:16, :],
                tab_scales[0].bitcast(I32).rearrange("(g e) c -> e g c", e=2)[e],
            )
        nc.scalar.dma_start(scale_window[:].bitcast(I32)[4:PARTS:8, :], tab_scales[1].bitcast(I32))
        nc.scalar.activation(warm_out[:], warm_in[:], ACT.Exp)

        w1_raw = {}

        def load_w1(a, b, pool, **place):
            raw = pool.tile([PARTS, PACK, K_PASS], F32, name="w1_raw%d%d" % (a, b), align_bytes=64, **place)
            nc.sync.dma_start(
                raw[:],
                w1[K_PASS * a : K_PASS * (a + 1), K_PASS * b : K_PASS * (b + 1)].rearrange("(p j) c -> p j c", j=PACK),
            )
            w1_raw[a, b] = raw

        w2_raw = keep.tile([PARTS, K_PASSES * H // 2], I32, name="w2_raw", tag="slot_c", align_bytes=64)
        nc.sync.dma_start(
            w2_raw[:].rearrange("p (a c) -> p a c", a=K_PASSES),
            w2_words.bitcast(I32).rearrange("a p c -> p a c"),
        )
        load_w1(0, 0, keep, tag="slot_d")
        w2s_raw = keep.tile([PARTS, K_PASSES * H // 4], I32, name="w2s_raw", align_bytes=64)
        nc.gpsimd.memset(w2s_raw[:], 0)
        for d in range(4):
            nc.gpsimd.dma_start(
                w2s_raw[32 * d : 32 * d + 4, :].rearrange("r (a c) -> r a c", a=K_PASSES),
                w2_scales.bitcast(I32)[:, 4 * d : 4 * d + 4, :].rearrange("a r c -> r a c"),
            )

        v_scales = [keep.tile([PARTS, S], U8, name="v_scales%d" % a, align_bytes=64) for a in range(K_PASSES)]
        nc.vector.memset(v_scales[1][:].bitcast(I32), 0)
        v_words = [
            keep.tile([PARTS, S], U32, name="v_words0", align_bytes=64),
            placed.tile([PARTS, S], U32, name="v_words1", offset=12288, align_bytes=64),
        ]
        nc.vector.tensor_copy(v_words[0][:], word_windows[0][:].bitcast(U32).indirect(offs_t[:]))
        load_w1(1, 0, placed, offset=0)
        picked_scales = placed.tile([PARTS, S], U8, name="picked_scales", offset=15360, align_bytes=64)
        nc.vector.tensor_copy(picked_scales[:], scale_window[:].indirect(offs_t[:]))
        staged = placed.tile([PARTS, S // 4], I32, name="staged", offset=24064, align_bytes=64)
        nc.vector.tensor_copy(staged[:], picked_scales[:].bitcast(I32))
        nc.vector.tensor_copy(v_scales[0][:].bitcast(I32), picked_scales[:].bitcast(I32))
        for r in range(4):
            nc.scalar.dma_start(v_scales[1][:].bitcast(I32)[r:PARTS:32, :], staged[8 * r + 4 : PARTS : 32, :])
        for e in range(2):
            nc.scalar.dma_start(v_scales[0][:].bitcast(I32)[2 + e : PARTS : 32, :], staged[16 + e : PARTS : 32, :])
        nc.vector.tensor_copy(v_words[1][:], word_windows[1][:].bitcast(U32).indirect(offs_t[:]))
        gain_t = keep.tile([PARTS, R_PASSES, 16], F32, name="gain_t", tag="slot_w1", align_bytes=64)
        for w in range(RUN):
            nc.sync.dma_start(
                gain_t[w:PARTS:RUN, :, 0:13],
                gain.rearrange("(b i x) -> i b x", b=R_PASSES, x=16)[:, :, w : w + 13],
            )

        w2_planes = keep.tile([PARTS, K_PASSES * H], U8, name="w2_planes", align_bytes=64)
        nc.vector.tensor_copy(
            w2_planes[:].bitcast(I32).rearrange("p (g t i x) -> p g i t x", t=PACK, i=8, x=4),
            w2s_raw[:].rearrange("p (g i x t) -> p g i t x", t=PACK, i=8, x=4),
        )
        w2_source = w2_raw[:].rearrange("p (a b i t x) -> p b t a i x", a=K_PASSES, b=R_PASSES, t=PACK, x=2)
        w2_codes = {}

        def deal_w2(tile, n0, n1):
            words = tile[:].bitcast(I32).rearrange("p (n a i x) -> p n a i x", a=K_PASSES, i=32, x=2)
            for b in range(R_PASSES):
                t0, t1 = max(n0 - PACK * b, 0), min(n1 - PACK * b, PACK)
                if t0 < t1:
                    nc.vector.tensor_copy(words[:, PACK * b + t0 - n0 : PACK * b + t1 - n0], w2_source[:, b, t0:t1])
            for n in range(n0, n1):
                for a in range(K_PASSES):
                    c0 = 2 * PARTS * (K_PASSES * (n - n0) + a)
                    w2_codes[n, a] = tile[:, c0 : c0 + 2 * PARTS]

        deal_w2(keep.tile([PARTS, K_PASSES * 2 * PARTS], U8, name="w2_first", align_bytes=64), 0, 1)
        load_w1(0, 1, placed, offset=16384)
        load_w1(1, 1, placed, offset=24576)

        w3_raw = {}

        def load_w3(b, pool, **place):
            raw = pool.tile([PARTS, PACK, N], F32, name="w3_raw%d" % b, align_bytes=64, **place)
            rows = w3[K_PASS * b : K_PASS * (b + 1), :].rearrange("(i t w) n -> w i t n", t=PACK, w=RUN)
            for w in range(RUN):
                nc.sync.dma_start(raw[w:PARTS:RUN, :, :], rows[w])
            w3_raw[b] = raw

        w1_grouped = [keep.tile([PARTS, K_PASSES * K_PASS], BF16, name="w1_grouped%d" % n, tag="grouped%d" % n, align_bytes=64) for n in range(TILES)]
        w1_q = {}

        def round_w1(a, n, copy):
            b, t = divmod(n, PACK)
            copy(
                w1_grouped[n][:, K_PASS * a : K_PASS * (a + 1)].rearrange("p (i w j) -> p i j w", w=RUN, j=PACK),
                w1_raw[a, b][:].rearrange("p j (i t w) -> p t i j w", t=PACK, w=RUN)[:, t],
            )

        def quantise_w1(n):
            codes = work.tile([PARTS, K_PASSES * PARTS], U32, name="w1_codes", bufs=4, align_bytes=64)
            scales = work.tile([PARTS, K_PASSES * PARTS], U8, name="w1_scales", bufs=4, align_bytes=64)
            nc.vector.quantize_mx(out=codes[:].bitcast(FP8X4), scales=scales[:], in_=w1_grouped[n][:])
            w1_q[n] = (codes, scales)

        halves = [slice(BANK * half, BANK * (half + 1)) for half in range(S // BANK)]
        tanh_b = {}

        def bounded_part(n):
            if n == 0:
                tanh_b[n] = keep.tile([PARTS, S], F32, name="tanh_first", tag="slot_d", align_bytes=64)
            else:
                tanh_b[n] = work.tile([PARTS, S], F32, name="tanh_b")
            for cols in halves:
                bank = psum.tile([PARTS, BANK], F32, name="bounded", bufs=4)
                for a in range(K_PASSES):
                    c0 = PARTS * (TILES * a + n)
                    nc.tensor.matmul_mx(
                        out=bank[:],
                        lhsT=w2_codes[n, a].bitcast(FP4X4),
                        lhsT_scale=w2_planes[:, c0 : c0 + PARTS],
                        rhs=v_words[a][:, cols].bitcast(FP8X4),
                        rhs_scale=v_scales[a][:, cols],
                        start=(a == 0),
                        stop=(a == K_PASSES - 1),
                    )
                nc.scalar.activation(tanh_b[n][:, cols], bank[:], ACT.Tanh)

        h_tiles = {}
        opposite = {}

        def features(n, pair_ranges):
            codes, scales = w1_q[n]
            h = work.tile([PARTS, S], F32, name="h", bufs=3)
            for cols in halves:
                bank = psum.tile([PARTS, BANK], F32, name="linear", bufs=4)
                for a in range(K_PASSES):
                    nc.tensor.matmul_mx(
                        out=bank[:],
                        lhsT=codes[:, PARTS * a : PARTS * (a + 1)].bitcast(FP8X4),
                        lhsT_scale=scales[:, PARTS * a : PARTS * (a + 1)],
                        rhs=v_words[a][:, cols].bitcast(FP8X4),
                        rhs_scale=v_scales[a][:, cols],
                        start=(a == 0),
                        stop=(a == K_PASSES - 1),
                    )
                nc.vector.tensor_tensor(h[:, cols], bank[:], tanh_b[n][:, cols], ALU.add)
            h_tiles[n] = h
            for m0, m1 in pair_ranges:
                h2 = work.tile([PARTS, m1 - m0], F32, name="h2", bufs=3)
                nc.vector.tensor_copy(h2[:], h[:].indirect(pos2_t[:, m0 // 16 : m1 // 16]))
                opposite[n, m0] = h2

        z_f32 = [keep.tile([PARTS, PACK * P], F32, name="z_f32_%d" % b) for b in range(R_PASSES)]

        def damp(n, pair_ranges):
            b, t = divmod(n, PACK)
            for m0, m1 in pair_ranges:
                size = work.tile([PARTS, m1 - m0], F32, name="size")
                nc.scalar.activation(size[:], opposite[n, m0][:], ACT.Abs)
                decay = work.tile([PARTS, m1 - m0], F32, name="decay")
                nc.scalar.activation(decay[:], size[:], ACT.Exp, scale=-1.0)
                factor = work.tile([PARTS, m1 - m0], F32, name="factor")
                nc.scalar.activation(factor[:], decay[:], ACT.Copy, scale=gain_t[:, b, RUN * t : RUN * t + 1])
                nc.vector.tensor_tensor(
                    z_f32[b][:, P * t + m0 : P * t + m1],
                    h_tiles[n][:].indirect(pos1_t[:, m0 // 16 : m1 // 16]),
                    factor[:],
                    ALU.mult,
                )

        w3_grouped = [keep.tile([PARTS, N * PACK], BF16, name="w3_grouped%d" % b, align_bytes=64) for b in range(R_PASSES)]
        w3_q = {}

        def round_w3(b, k):
            nc.scalar.copy(
                w3_grouped[b][:, K_PASS * k : K_PASS * (k + 1)].rearrange("p (c x t) -> p c t x", x=4, t=PACK),
                w3_raw[b][:, :, PARTS * k : PARTS * (k + 1)].rearrange("p t (c x) -> p c t x", x=4),
            )

        def quantise_w3(b):
            codes = work.tile([PARTS, N], U32, name="w3_codes", align_bytes=64)
            scales = work.tile([PARTS, N], U8, name="w3_scales", align_bytes=64)
            for c0, c1 in ((0, 256), (256, N)):
                nc.vector.quantize_mx(
                    out=codes[:, c0:c1].bitcast(FP8X4), scales=scales[:, c0:c1], in_=w3_grouped[b][:, PACK * c0 : PACK * c1]
                )
            w3_q[b] = (codes, scales)

        z_grouped = [keep.tile([PARTS, P * PACK], BF16, name="z_grouped%d" % b, align_bytes=64) for b in range(R_PASSES)]
        z_codes = [keep.tile([PARTS, P], U32, name="z_codes%d" % b, align_bytes=64) for b in range(R_PASSES)]
        z_scales = [keep.tile([PARTS, P], U8, name="z_scales%d" % b, align_bytes=64) for b in range(R_PASSES)]

        def round_z(b, m0, m1, copy):
            copy(
                z_grouped[b][:, PACK * m0 : PACK * m1].rearrange("p (c x t) -> p c t x", x=4, t=PACK),
                z_f32[b][:].rearrange("p (t m) -> p t m", t=PACK)[:, :, m0:m1].rearrange("p t (c x) -> p c t x", x=4),
            )

        def quantise_z(b, m0, m1):
            nc.vector.quantize_mx(
                out=z_codes[b][:, m0:m1].bitcast(FP8X4), scales=z_scales[b][:, m0:m1], in_=z_grouped[b][:, PACK * m0 : PACK * m1]
            )

        def second_product(scores, b, m0, m1):
            for k in range(N_TILES):
                cols = slice(PARTS * k, PARTS * (k + 1))
                nc.tensor.matmul_mx(
                    out=scores[k][:, 0 : m1 - m0],
                    lhsT=w3_q[b][0][:, cols].bitcast(FP8X4),
                    lhsT_scale=w3_q[b][1][:, cols],
                    rhs=z_codes[b][:, m0:m1].bitcast(FP8X4),
                    rhs_scale=z_scales[b][:, m0:m1],
                    start=(b == 0),
                    stop=(b == R_PASSES - 1),
                )

        def store(scores, m0, m1, copies):
            for k in range(N_TILES):
                result = work.tile([PARTS, m1 - m0], F32, name="result", bufs=2 * N_TILES)
                copies[k](result[:], scores[k][:, 0 : m1 - m0])
                nc.sync.dma_start(out[PARTS * k : PARTS * (k + 1), m0:m1], result[:])

        whole = [(0, P)]
        split = [(0, P // 2), (P // 2, P)]
        last = TILES - 1

        for n in range(PACK):
            round_w1(0, n, nc.scalar.copy)
        bounded_part(0)
        for n in range(2):
            round_w1(1, n, nc.vector.tensor_copy)
            quantise_w1(n)
            if n == 0:
                rest = keep.tile([PARTS, (TILES - 1) * K_PASSES * 2 * PARTS], U8, name="w2_rest", tag="grouped0", align_bytes=64)
                deal_w2(rest, 1, TILES)
        for n in range(2, PACK):
            round_w1(1, n, nc.scalar.copy)
        features(0, whole)
        for n in range(2, PACK):
            quantise_w1(n)
        bounded_part(1)
        load_w3(0, keep, tag="slot_c")
        load_w3(1, placed, offset=0)
        features(1, whole)
        for n in range(2, TILES):
            damp(n - 2, whole)
            bounded_part(n)
            features(n, split if n == last else whole)
            if n + 2 < TILES:
                for a in range(K_PASSES):
                    round_w1(a, n + 2, nc.scalar.copy)
                quantise_w1(n + 2)
            if n >= last - 1:
                for k in range(N_TILES):
                    round_w3(n - last + 1, k)
                quantise_w3(n - last + 1)
        round_z(0, P // 2, P, nc.vector.tensor_copy)
        damp(last - 1, whole)
        scores = [
            [psum.tile([PARTS, BANK], F32, name="scores_%s%d" % (tag, k), tag=tag, bufs=4) for k in range(N_TILES)]
            for tag in ("bounded", "linear")
        ]
        round_z(0, 0, P // 2, nc.scalar.copy)
        quantise_z(0, 0, P)
        for half, (m0, m1) in enumerate(split):
            second_product(scores[half], 0, m0, m1)
        damp(last, split)
        round_z(1, 0, P // 2, nc.scalar.copy)
        round_z(1, P // 2, P, nc.vector.tensor_copy)
        for half, (m0, m1) in enumerate(split):
            quantise_z(1, m0, m1)
            second_product(scores[half], 1, m0, m1)
        store(scores[0], 0, P // 2, (nc.scalar.copy, nc.scalar.copy, nc.vector.tensor_copy))
        store(scores[1], P // 2, P, (nc.vector.tensor_copy, nc.scalar.copy, nc.vector.tensor_copy))
